import numpy as np
import ml_dtypes


def mxq(x, axis, fmt="e4m3"):
    dtype, down = {"e4m3": (ml_dtypes.float8_e4m3fn, 7), "e5m2": (ml_dtypes.float8_e5m2, 14)}[fmt]
    v = np.moveaxis(np.asarray(x, np.float32).astype(ml_dtypes.bfloat16).astype(np.float64), axis, -1)
    blocks = v.reshape(v.shape[:-1] + (-1, 32))
    amax = np.abs(blocks).max(-1, keepdims=True)
    byte = np.maximum(np.where(amax > 0, np.frexp(amax)[1] - 1 + 127, 0) - down, 1)
    scale = np.exp2(byte - 127.0)
    codes = (blocks / scale).astype(np.float32).astype(dtype).astype(np.float64)
    return np.moveaxis((codes * scale).reshape(v.shape), -1, axis)


WIDE = False


def mx_kscale(k):
    if not WIDE:
        return np.ones(k)
    levels = np.array([10, -10, 5, -5, 0])
    if k % 512:
        return np.exp2(np.random.permutation(np.resize(levels, k // 32))).repeat(32)
    a = np.empty((k // 512, 16))
    for p in range(k // 512):
        a[p, :8] = np.random.permutation(np.resize(levels, 8))
        for g in range(8):
            far = levels[np.abs(levels - a[p, g]) >= 10]
            a[p, g + 8] = far[np.random.randint(len(far))]
    return np.exp2(a.ravel()).repeat(32)


def f64(x):
    return np.asarray(x).astype(np.float64)


def striped(idx):
    return np.tile(idx.reshape(-1, 16).T, (8, 1)).astype(np.uint16)


def unstriped(offs):
    return offs[:16].T.reshape(-1).astype(np.int64)


def striped8(idx):
    return np.concatenate([x.reshape(-1, 16).T for x in idx]).astype(np.uint16)


def runs(offs, k):
    lists = np.stack([offs[16 * r : 16 * r + 16].T.reshape(-1) for r in range(8)]).astype(np.int64)
    return lists[np.arange(k) % 512 // 64]


def pack_weight(w):
    k, n = w.shape
    w = f64(np.asarray(w, np.float32).astype(ml_dtypes.bfloat16)).reshape(k // 32, 32, n)
    amax = np.abs(w).max(1)
    byte = np.clip(np.where(amax > 0, np.frexp(amax)[1] - 1 + 127 - 7, 1), 1, 254)
    scaled = (w * np.exp2(127.0 - byte)[:, None, :]).reshape(k, n).astype(np.float32)
    words = np.ascontiguousarray(scaled.reshape(k // 512, 128, 4, n).transpose(0, 1, 3, 2)).astype(ml_dtypes.float8_e4m3fn).view(np.uint8)
    return words, np.ascontiguousarray(byte.astype(np.uint8).reshape(k // 512, 16, n))


def unpack_weight(words, scales):
    g, p, n, _ = words.shape
    vals = np.ascontiguousarray(words).view(ml_dtypes.float8_e4m3fn).astype(np.float64) * np.repeat(np.exp2(scales.astype(np.float64) - 127.0), 8, axis=1)[..., None]
    return vals.transpose(0, 1, 3, 2).reshape(g * 512, n)


K, T, S, H = 512, 2048, 512, 512


def setup_inputs():
    n = np.random.standard_normal
    s = mx_kscale(K)[:, None]
    u = mx_kscale(S)
    packed_xT = pack_weight(n((K, T)) * s)
    return {
        "x_words": packed_xT[0],
        "x_scales": packed_xT[1],
        "w1": (n((K, H)) / np.sqrt(K) / s).astype(np.float32),
        "ga": (np.random.uniform(0.5, 1.5, (H, 1)) * u[:, None]).astype(np.float32),
        "gb": (np.random.uniform(0.5, 1.5, (H, 1)) / u[:, None]).astype(np.float32),
        "offs": striped(np.random.permutation(T)[:S]),
        "n1": striped8(np.stack([np.random.permutation(S) for _ in range(8)])),
        "n2": striped8(np.stack([np.random.permutation(S) for _ in range(8)])),
        "n3": striped8(np.stack([np.random.permutation(S) for _ in range(8)])),
        "n4": striped8(np.stack([np.random.permutation(S) for _ in range(8)])),
        "n5": striped8(np.stack([np.random.permutation(S) for _ in range(8)])),
        "n6": striped8(np.stack([np.random.permutation(S) for _ in range(8)])),
        "n7": striped8(np.stack([np.random.permutation(S) for _ in range(8)])),
    }


def reference(x_words, x_scales, w1, ga, gb, offs, n1, n2, n3, n4, n5, n6, n7):
    xq = unpack_weight(x_words, x_scales)[:, unstriped(offs)]
    y = mxq(f64(w1), 0, "e4m3").T @ xq
    z = f64(ga) * ((y[np.arange(H)[:, None], runs(n1, H)]) * (y[np.arange(H)[:, None], runs(n2, H)]))
    b1 = y[np.arange(H)[:, None], runs(n3, H)]
    b2 = y[np.arange(H)[:, None], runs(n4, H)]
    b3 = y[np.arange(H)[:, None], runs(n5, H)]
    z2 = f64(gb) * (np.maximum(np.maximum(b1, b2), b3) - (0.5 * (np.maximum(np.minimum(b1, b2), np.minimum(np.maximum(b1, b2), b3)))))
    s = 0.0625 * ((mxq(z, 0, "e4m3").T @ mxq(z2, 0, "e4m3")))
    pa = s[np.arange(S)[:, None], runs(n6, S)]
    pb = s[np.arange(S)[:, None], runs(n7, S)]
    return np.maximum(np.minimum(s, pa), np.minimum(np.maximum(s, pa), pb))

@@ -1,0 +1,189 @@
+from contextlib import ExitStack
+
+import concourse.mybir as mybir
+
+K, T, S, H = 512, 2048, 512, 512
+FLOPS = 2 * K * H * S + 2 * H * S * S
+
+F32 = mybir.dt.float32
+BF16 = mybir.dt.bfloat16
+I32 = mybir.dt.int32
+U32 = mybir.dt.uint32
+U16 = mybir.dt.uint16
+U8 = mybir.dt.uint8
+FP8X4 = mybir.dt.float8_e4m3fn_x4
+ALU = mybir.AluOpType
+COPY = mybir.ActivationFunctionType.Copy
+
+P = 128
+PACK = 4
+HALF = S // 2
+LANES = 16
+
+
+def tile_picked_selfprodtop2med_none_p_kernel(
+    tc, x_words, x_scales, w1, ga, gb, offs, n1, n2, n3, n4, n5, n6, n7, out
+):
+    nc = tc.nc
+    with ExitStack() as ctx:
+        keep = ctx.enter_context(tc.tile_pool(name="keep", bufs=1))
+        psum = ctx.enter_context(tc.psum_pool(name="psum", bufs=1))
+
+        def sb(name, shape, dtype):
+            return keep.tile(shape, dtype, name=name, align_bytes=64)
+
+        def load_list(name, src):
+            lst = sb(name, [P, S // LANES], U16)
+            nc.sync.dma_start(lst[:], src)
+            return lst
+
+        def gather(engine, dst, window, lst, h):
+            picked = window[:].indirect(lst[:, h * HALF // LANES : (h + 1) * HALF // LANES])
+            if engine == "scalar":
+                nc.scalar.activation(dst, picked, COPY)
+            else:
+                nc.vector.tensor_copy(dst, picked)
+
+        xs = sb("xs", [P, T], U8)
+        nc.vector.memset(xs[:].bitcast(I32), 0)
+        w_raw = sb("w_raw", [P, PACK, H], F32)
+        nc.sync.dma_start(w_raw[:], w1.rearrange("(p j) c -> p j c", j=PACK))
+        l_offs = load_list("l_offs", offs)
+        for q in range(4):
+            nc.scalar.dma_start(xs[32 * q : 32 * q + 4, :].bitcast(I32), x_scales[0, 4 * q : 4 * q + 4, :].bitcast(I32))
+        xw = sb("xw", [P, T], U32)
+        nc.sync.dma_start(xw[:].bitcast(I32), x_words[0].rearrange("p n r -> p (n r)").bitcast(I32))
+        ga_sb = sb("ga_sb", [P, PACK], F32)
+        gb_sb = sb("gb_sb", [P, PACK], F32)
+        nc.gpsimd.dma_start(gb_sb[:], gb.rearrange("(p t) o -> p (t o)", t=PACK))
+        nc.gpsimd.dma_start(ga_sb[:], ga.rearrange("(p t) o -> p (t o)", t=PACK))
+        l3 = load_list("l3", n3)
+        l4 = load_list("l4", n4)
+        l5 = load_list("l5", n5)
+        l1 = load_list("l1", n1)
+        l2 = load_list("l2", n2)
+        l6 = load_list("l6", n6)
+        l7 = load_list("l7", n7)
+
+        w_bf = sb("w_bf", [P, H * PACK], BF16)
+        nc.vector.tensor_copy(
+            w_bf[:].rearrange("p (t m j) -> p m j t", t=PACK, j=PACK),
+            w_raw[:].rearrange("p j (m t) -> p m j t", t=PACK),
+        )
+        xs_pick = sb("xs_pick", [P, S], U8)
+        nc.vector.tensor_copy(xs_pick[:], xs[:].indirect(l_offs[:]))
+        w_codes = sb("w_codes", [P, H], U32)
+        w_scales = sb("w_scales", [P, H], U8)
+        nc.vector.quantize_mx(out=w_codes[:].bitcast(FP8X4), scales=w_scales[:], in_=w_bf[:])
+        xw_pick = sb("xw_pick", [P, S], U32)
+        nc.vector.tensor_copy(xw_pick[:], xw[:].indirect(l_offs[:]))
+
+        y = []
+        for t in range(PACK):
+            acc = psum.tile([P, S], F32, name="y_acc%d" % t)
+            cols = slice(t * P, (t + 1) * P)
+            nc.tensor.matmul_mx(
+                out=acc[:], lhsT=w_codes[:, cols].bitcast(FP8X4), lhsT_scale=w_scales[:, cols],
+                rhs=xw_pick[:].bitcast(FP8X4), rhs_scale=xs_pick[:], start=True, stop=True,
+            )
+            y_t = sb("y%d" % t, [P, S], F32)
+            if t % 2 == 0:
+                nc.scalar.copy(y_t[:], acc[:])
+            else:
+                nc.vector.tensor_copy(y_t[:], acc[:])
+            y.append(y_t)
+
+        z2_bf = sb("z2_bf", [P, S * PACK], BF16)
+        z2_codes = sb("z2_codes", [P, S], U32)
+        z2_scales = sb("z2_scales", [P, S], U8)
+        gb_wide = gb_sb[:].rearrange("p (c t i) -> p c t i", c=1, i=1).to_broadcast([P, HALF // 4, PACK, 4])
+        for h in range(2):
+            b1 = sb("b1_%d" % h, [P, PACK, HALF], F32)
+            b2 = sb("b2_%d" % h, [P, PACK, HALF], F32)
+            b3 = sb("b3_%d" % h, [P, PACK, HALF], F32)
+            for t in range(PACK):
+                gather("scalar", b1[:, t, :], y[t], l3, h)
+                gather("vector" if h == 0 else "scalar", b2[:, t, :], y[t], l4, h)
+            for t in range(PACK):
+                gather("scalar", b3[:, t, :], y[t], l5, h)
+            hi = sb("hi_%d" % h, [P, PACK, HALF], F32)
+            lo = sb("lo_%d" % h, [P, PACK, HALF], F32)
+            top = sb("top_%d" % h, [P, PACK, HALF], F32)
+            cut = sb("cut_%d" % h, [P, PACK, HALF], F32)
+            med = sb("med_%d" % h, [P, PACK, HALF], F32)
+            mix = sb("mix_%d" % h, [P, PACK, HALF], F32)
+            pairs = [slice(0, 2), slice(2, 4)]
+            for u in pairs:
+                nc.vector.tensor_tensor(hi[:, u, :], b1[:, u, :], b2[:, u, :], ALU.max)
+                nc.vector.tensor_tensor(lo[:, u, :], b1[:, u, :], b2[:, u, :], ALU.min)
+            for u in pairs:
+                nc.vector.tensor_tensor(cut[:, u, :], hi[:, u, :], b3[:, u, :], ALU.min)
+                nc.vector.tensor_tensor(top[:, u, :], hi[:, u, :], b3[:, u, :], ALU.max)
+            for u in pairs:
+                nc.vector.tensor_tensor(med[:, u, :], lo[:, u, :], cut[:, u, :], ALU.max)
+            for u in pairs:
+                nc.vector.scalar_tensor_tensor(mix[:, u, :], med[:, u, :], -0.5, top[:, u, :], ALU.mult, ALU.add)
+            half_bf = z2_bf[:, h * HALF * PACK : (h + 1) * HALF * PACK]
+            nc.vector.tensor_tensor(
+                half_bf.rearrange("p (c i t) -> p c t i", i=4, t=PACK),
+                mix[:].rearrange("p t (c i) -> p c t i", i=4),
+                gb_wide,
+                ALU.mult,
+            )
+            cols = slice(h * HALF, (h + 1) * HALF)
+            nc.vector.quantize_mx(out=z2_codes[:, cols].bitcast(FP8X4), scales=z2_scales[:, cols], in_=half_bf)
+
+        z_bf = sb("z_bf", [P, PACK, P * PACK], BF16)
+        for h in range(2):
+            a1 = sb("a1_%d" % h, [P, PACK, HALF], F32)
+            a2 = sb("a2_%d" % h, [P, PACK, HALF], F32)
+            z_rows = sb("z_rows_%d" % h, [P, PACK, HALF], BF16)
+            for t in range(PACK):
+                gather("scalar", a1[:, t, :], y[t], l1, h)
+                gather("scalar", a2[:, t, :], y[t], l2, h)
+                nc.vector.scalar_tensor_tensor(z_rows[:, t, :], a1[:, t, :], ga_sb[:, t : t + 1], a2[:, t, :], ALU.mult, ALU.mult)
+            nc.vector.tensor_copy(
+                z_bf[:, :, h * HALF : (h + 1) * HALF].rearrange("p i (c e t) -> p c t e i", e=2, t=PACK),
+                z_rows[:].rearrange("p t (c e i) -> p c t e i", e=2, i=4),
+            )
+
+        z_codes = sb("z_codes", [P, S], U32)
+        z_scales = sb("z_scales", [P, S], U8)
+        s = []
+        for t in range(PACK):
+            cols = slice(t * P, (t + 1) * P)
+            nc.vector.quantize_mx(out=z_codes[:, cols].bitcast(FP8X4), scales=z_scales[:, cols], in_=z_bf[:, t, :])
+        for t in range(PACK):
+            cols = slice(t * P, (t + 1) * P)
+            acc = psum.tile([P, S], F32, name="s_acc%d" % t)
+            nc.tensor.matmul_mx(
+                out=acc[:], lhsT=z_codes[:, cols].bitcast(FP8X4), lhsT_scale=z_scales[:, cols],
+                rhs=z2_codes[:].bitcast(FP8X4), rhs_scale=z2_scales[:], start=True, stop=True,
+            )
+            s_t = sb("s%d" % t, [P, S], F32)
+            if t == 0:
+                nc.scalar.activation(s_t[:], acc[:], COPY, scale=0.0625)
+            else:
+                nc.vector.tensor_scalar(s_t[:], acc[:], 0.0625, None, ALU.mult)
+            s.append(s_t)
+
+        out_rows = out.rearrange("(p t) j -> t p j", t=PACK)
+        halves = [slice(0, HALF), slice(HALF, S)]
+        for t in range(PACK):
+            pa = sb("pa%d" % t, [P, S], F32)
+            pb = sb("pb%d" % t, [P, S], F32)
+            for h in range(2):
+                gather("scalar", pa[:, halves[h]], s[t], l6, h)
+            for h in range(2):
+                gather("scalar", pb[:, halves[h]], s[t], l7, h)
+            s_hi = sb("s_hi%d" % t, [P, S], F32)
+            s_lo = sb("s_lo%d" % t, [P, S], F32)
+            s_cut = sb("s_cut%d" % t, [P, S], F32)
+            res = sb("res%d" % t, [P, S], F32)
+            nc.vector.tensor_tensor(s_hi[:], s[t][:], pa[:], ALU.max)
+            nc.vector.tensor_tensor(s_lo[:], s[t][:], pa[:], ALU.min)
+            for c in halves:
+                nc.vector.tensor_tensor(s_cut[:, c], s_hi[:, c], pb[:, c], ALU.min)
+            for c in halves:
+                nc.vector.tensor_tensor(res[:, c], s_lo[:, c], s_cut[:, c], ALU.max)
+                nc.sync.dma_start(out_rows[t][:, c], res[:, c])

@@ -19,6 +19,8 @@ P = 128
 PACK = 4
 HALF = S // 2
 LANES = 16
+WINDOW = 2 * S
+W_SPLIT = 64
 
 
 def tile_picked_selfprodtop2med_none_p_kernel(
@@ -37,153 +39,198 @@ def tile_picked_selfprodtop2med_none_p_kernel(
             nc.sync.dma_start(lst[:], src)
             return lst
 
-        def gather(engine, dst, window, lst, h):
-            picked = window[:].indirect(lst[:, h * HALF // LANES : (h + 1) * HALF // LANES])
+        def gather(engine, dst, window, lst, cols):
+            picked = window[:].indirect(lst[:, cols.start // LANES : cols.stop // LANES])
             if engine == "scalar":
                 nc.scalar.activation(dst, picked, COPY)
             else:
                 nc.vector.tensor_copy(dst, picked)
 
+        whole = slice(0, S)
+        halves = [slice(0, HALF), slice(HALF, S)]
+
         xs = sb("xs", [P, T], U8)
-        nc.vector.memset(xs[:].bitcast(I32), 0)
+        nc.gpsimd.memset(xs[:].bitcast(U32), 0)
         w_raw = sb("w_raw", [P, PACK, H], F32)
         nc.sync.dma_start(w_raw[:], w1.rearrange("(p j) c -> p j c", j=PACK))
-        l_offs = load_list("l_offs", offs)
         for q in range(4):
-            nc.scalar.dma_start(xs[32 * q : 32 * q + 4, :].bitcast(I32), x_scales[0, 4 * q : 4 * q + 4, :].bitcast(I32))
+            nc.sync.dma_start(xs[32 * q : 32 * q + 4, :].bitcast(I32), x_scales[0, 4 * q : 4 * q + 4, :].bitcast(I32))
+        l_offs = load_list("l_offs", offs)
         xw = sb("xw", [P, T], U32)
         nc.sync.dma_start(xw[:].bitcast(I32), x_words[0].rearrange("p n r -> p (n r)").bitcast(I32))
-        ga_sb = sb("ga_sb", [P, PACK], F32)
-        gb_sb = sb("gb_sb", [P, PACK], F32)
-        nc.gpsimd.dma_start(gb_sb[:], gb.rearrange("(p t) o -> p (t o)", t=PACK))
-        nc.gpsimd.dma_start(ga_sb[:], ga.rearrange("(p t) o -> p (t o)", t=PACK))
         l3 = load_list("l3", n3)
         l4 = load_list("l4", n4)
         l5 = load_list("l5", n5)
         l1 = load_list("l1", n1)
         l2 = load_list("l2", n2)
+        ga_sb = sb("ga_sb", [P, PACK], F32)
+        gb_sb = sb("gb_sb", [P, PACK], F32)
+        nc.sync.dma_start(gb_sb[:], gb.rearrange("(p t) o -> p (t o)", t=PACK))
+        nc.sync.dma_start(ga_sb[:], ga.rearrange("(p t) o -> p (t o)", t=PACK))
         l6 = load_list("l6", n6)
         l7 = load_list("l7", n7)
 
+        y = [sb("y%d" % t, [P, WINDOW], F32) for t in range(PACK)]
+        s = [sb("s%d" % t, [P, WINDOW], F32) for t in range(PACK)]
+
         w_bf = sb("w_bf", [P, H * PACK], BF16)
-        nc.vector.tensor_copy(
-            w_bf[:].rearrange("p (t m j) -> p m j t", t=PACK, j=PACK),
-            w_raw[:].rearrange("p j (m t) -> p m j t", t=PACK),
-        )
+        w_dst = w_bf[:].rearrange("p (t m j) -> p m j t", t=PACK, j=PACK)
+        w_src = w_raw[:].rearrange("p j (m t) -> p m j t", t=PACK)
+        nc.vector.tensor_copy(w_dst[:, :W_SPLIT], w_src[:, :W_SPLIT])
+        nc.scalar.copy(w_dst[:, W_SPLIT:], w_src[:, W_SPLIT:])
         xs_pick = sb("xs_pick", [P, S], U8)
         nc.vector.tensor_copy(xs_pick[:], xs[:].indirect(l_offs[:]))
         w_codes = sb("w_codes", [P, H], U32)
         w_scales = sb("w_scales", [P, H], U8)
         nc.vector.quantize_mx(out=w_codes[:].bitcast(FP8X4), scales=w_scales[:], in_=w_bf[:])
         xw_pick = sb("xw_pick", [P, S], U32)
-        nc.vector.tensor_copy(xw_pick[:], xw[:].indirect(l_offs[:]))
+        for c in halves:
+            gather("vector", xw_pick[:, c], xw, l_offs, c)
 
-        y = []
-        for t in range(PACK):
-            acc = psum.tile([P, S], F32, name="y_acc%d" % t)
+        def product(acc, codes, scales, t, rhs, rhs_scales, c):
             cols = slice(t * P, (t + 1) * P)
             nc.tensor.matmul_mx(
-                out=acc[:], lhsT=w_codes[:, cols].bitcast(FP8X4), lhsT_scale=w_scales[:, cols],
-                rhs=xw_pick[:].bitcast(FP8X4), rhs_scale=xs_pick[:], start=True, stop=True,
+                out=acc, lhsT=codes[:, cols].bitcast(FP8X4), lhsT_scale=scales[:, cols],
+                rhs=rhs[:, c].bitcast(FP8X4), rhs_scale=rhs_scales[:, c], start=True, stop=True,
             )
-            y_t = sb("y%d" % t, [P, S], F32)
-            if t % 2 == 0:
-                nc.scalar.copy(y_t[:], acc[:])
-            else:
-                nc.vector.tensor_copy(y_t[:], acc[:])
-            y.append(y_t)
+
+        def bank(b, width):
+            return psum.tile([P, width], F32, name="bank%d" % b, tag="bank%d" % b)
+
+        for h in range(2):
+            for t in range(2):
+                acc = bank(2 * h + t, HALF)
+                product(acc[:], w_codes, w_scales, t, xw_pick, xs_pick, halves[h])
+                if t == 0:
+                    nc.scalar.copy(y[t][:, halves[h]], acc[:])
+                else:
+                    nc.vector.tensor_copy(y[t][:, halves[h]], acc[:])
+        y_acc = {}
+        for t in range(2, PACK):
+            y_acc[t] = bank(2 + t, S)
+            product(y_acc[t][:], w_codes, w_scales, t, xw_pick, xs_pick, whole)
 
         z2_bf = sb("z2_bf", [P, S * PACK], BF16)
         z2_codes = sb("z2_codes", [P, S], U32)
         z2_scales = sb("z2_scales", [P, S], U8)
-        gb_wide = gb_sb[:].rearrange("p (c t i) -> p c t i", c=1, i=1).to_broadcast([P, HALF // 4, PACK, 4])
-        for h in range(2):
-            b1 = sb("b1_%d" % h, [P, PACK, HALF], F32)
-            b2 = sb("b2_%d" % h, [P, PACK, HALF], F32)
-            b3 = sb("b3_%d" % h, [P, PACK, HALF], F32)
-            for t in range(PACK):
-                gather("scalar", b1[:, t, :], y[t], l3, h)
-                gather("vector" if h == 0 else "scalar", b2[:, t, :], y[t], l4, h)
-            for t in range(PACK):
-                gather("scalar", b3[:, t, :], y[t], l5, h)
-            hi = sb("hi_%d" % h, [P, PACK, HALF], F32)
-            lo = sb("lo_%d" % h, [P, PACK, HALF], F32)
-            top = sb("top_%d" % h, [P, PACK, HALF], F32)
-            cut = sb("cut_%d" % h, [P, PACK, HALF], F32)
-            med = sb("med_%d" % h, [P, PACK, HALF], F32)
-            mix = sb("mix_%d" % h, [P, PACK, HALF], F32)
-            pairs = [slice(0, 2), slice(2, 4)]
-            for u in pairs:
-                nc.vector.tensor_tensor(hi[:, u, :], b1[:, u, :], b2[:, u, :], ALU.max)
-                nc.vector.tensor_tensor(lo[:, u, :], b1[:, u, :], b2[:, u, :], ALU.min)
-            for u in pairs:
-                nc.vector.tensor_tensor(cut[:, u, :], hi[:, u, :], b3[:, u, :], ALU.min)
-                nc.vector.tensor_tensor(top[:, u, :], hi[:, u, :], b3[:, u, :], ALU.max)
-            for u in pairs:
-                nc.vector.tensor_tensor(med[:, u, :], lo[:, u, :], cut[:, u, :], ALU.max)
-            for u in pairs:
-                nc.vector.scalar_tensor_tensor(mix[:, u, :], med[:, u, :], -0.5, top[:, u, :], ALU.mult, ALU.add)
-            half_bf = z2_bf[:, h * HALF * PACK : (h + 1) * HALF * PACK]
-            nc.vector.tensor_tensor(
-                half_bf.rearrange("p (c i t) -> p c t i", i=4, t=PACK),
-                mix[:].rearrange("p t (c i) -> p c t i", i=4),
-                gb_wide,
-                ALU.mult,
-            )
-            cols = slice(h * HALF, (h + 1) * HALF)
-            nc.vector.quantize_mx(out=z2_codes[:, cols].bitcast(FP8X4), scales=z2_scales[:, cols], in_=half_bf)
+        gb_wide = gb_sb[:].rearrange("p (c t i) -> p c t i", c=1, i=1).to_broadcast([P, S // 4, PACK, 4])
+        b1 = sb("b1", [P, PACK, S], F32)
+        b2 = sb("b2", [P, PACK, S], F32)
+        b3 = sb("b3", [P, PACK, S], F32)
+        hi = sb("hi", [P, PACK, S], F32)
+        lo = sb("lo", [P, PACK, S], F32)
+        top = sb("top", [P, PACK, S], F32)
+        cut = sb("cut", [P, PACK, S], F32)
+        med = sb("med", [P, PACK, S], F32)
+        mix = sb("mix", [P, PACK, S], F32)
+
+        def fetch(t):
+            gather("scalar", b1[:, t, :], y[t], l3, whole)
+            gather("vector" if t < 2 else "scalar", b2[:, t, :], y[t], l4, whole)
+            gather("scalar", b3[:, t, :], y[t], l5, whole)
+
+        def sort_pair(t):
+            nc.vector.tensor_tensor(hi[:, t, :], b1[:, t, :], b2[:, t, :], ALU.max)
+            nc.vector.tensor_tensor(lo[:, t, :], b1[:, t, :], b2[:, t, :], ALU.min)
+
+        def place_third(t):
+            nc.vector.tensor_tensor(cut[:, t, :], hi[:, t, :], b3[:, t, :], ALU.min)
+            nc.vector.tensor_tensor(top[:, t, :], hi[:, t, :], b3[:, t, :], ALU.max)
+
+        def median(t):
+            nc.vector.tensor_tensor(med[:, t, :], lo[:, t, :], cut[:, t, :], ALU.max)
+
+        def combine(t):
+            nc.vector.scalar_tensor_tensor(mix[:, t, :], med[:, t, :], -0.5, top[:, t, :], ALU.mult, ALU.add)
+
+        for t in range(PACK):
+            if t == 3:
+                nc.scalar.copy(y[3][:, :S], y_acc[3][:])
+            fetch(t)
+            sort_pair(t)
+            if t == 0:
+                nc.vector.tensor_copy(y[2][:, :S], y_acc[2][:])
+            else:
+                combine(t - 1)
+            place_third(t)
+            median(t)
 
         z_bf = sb("z_bf", [P, PACK, P * PACK], BF16)
-        for h in range(2):
-            a1 = sb("a1_%d" % h, [P, PACK, HALF], F32)
-            a2 = sb("a2_%d" % h, [P, PACK, HALF], F32)
-            z_rows = sb("z_rows_%d" % h, [P, PACK, HALF], BF16)
-            for t in range(PACK):
-                gather("scalar", a1[:, t, :], y[t], l1, h)
-                gather("scalar", a2[:, t, :], y[t], l2, h)
-                nc.vector.scalar_tensor_tensor(z_rows[:, t, :], a1[:, t, :], ga_sb[:, t : t + 1], a2[:, t, :], ALU.mult, ALU.mult)
-            nc.vector.tensor_copy(
-                z_bf[:, :, h * HALF : (h + 1) * HALF].rearrange("p i (c e t) -> p c t e i", e=2, t=PACK),
-                z_rows[:].rearrange("p t (c e i) -> p c t e i", e=2, i=4),
+        a1 = sb("a1", [P, PACK, S], F32)
+        a2 = sb("a2", [P, PACK, S], F32)
+        z_rows = sb("z_rows", [P, PACK, S], BF16)
+
+        def z_piece(t, c):
+            gather("scalar", a1[:, t, c], y[t], l1, c)
+            gather("scalar", a2[:, t, c], y[t], l2, c)
+            nc.vector.scalar_tensor_tensor(z_rows[:, t, c], a1[:, t, c], ga_sb[:, t : t + 1], a2[:, t, c], ALU.mult, ALU.mult)
+
+        def z_deal(copy, c):
+            copy(
+                z_bf[:, :, c].rearrange("p i (c e t) -> p c t e i", e=2, t=PACK),
+                z_rows[:, :, c].rearrange("p t (c e i) -> p c t e i", e=2, i=4),
             )
+
+        z_piece(0, whole)
+        combine(PACK - 1)
+        z_piece(1, whole)
+        nc.vector.tensor_tensor(
+            z2_bf[:].rearrange("p (c i t) -> p c t i", i=4, t=PACK),
+            mix[:].rearrange("p t (c i) -> p c t i", i=4),
+            gb_wide,
+            ALU.mult,
+        )
+        z_piece(2, whole)
+        nc.vector.quantize_mx(out=z2_codes[:].bitcast(FP8X4), scales=z2_scales[:], in_=z2_bf[:])
+        for c in halves:
+            z_piece(3, c)
+        z_deal(nc.scalar.copy, halves[0])
+        z_deal(nc.vector.tensor_copy, halves[1])
 
         z_codes = sb("z_codes", [P, S], U32)
         z_scales = sb("z_scales", [P, S], U8)
-        s = []
         for t in range(PACK):
             cols = slice(t * P, (t + 1) * P)
             nc.vector.quantize_mx(out=z_codes[:, cols].bitcast(FP8X4), scales=z_scales[:, cols], in_=z_bf[:, t, :])
-        for t in range(PACK):
-            cols = slice(t * P, (t + 1) * P)
-            acc = psum.tile([P, S], F32, name="s_acc%d" % t)
-            nc.tensor.matmul_mx(
-                out=acc[:], lhsT=z_codes[:, cols].bitcast(FP8X4), lhsT_scale=z_scales[:, cols],
-                rhs=z2_codes[:].bitcast(FP8X4), rhs_scale=z2_scales[:], start=True, stop=True,
-            )
-            s_t = sb("s%d" % t, [P, S], F32)
-            if t == 0:
-                nc.scalar.activation(s_t[:], acc[:], COPY, scale=0.0625)
+        def leave_psum(engine, dst, acc):
+            if engine == "scalar":
+                nc.scalar.activation(dst, acc[:], COPY, scale=0.0625)
             else:
-                nc.vector.tensor_scalar(s_t[:], acc[:], 0.0625, None, ALU.mult)
-            s.append(s_t)
+                nc.vector.tensor_scalar(dst, acc[:], 0.0625, None, ALU.mult)
+
+        for h in range(2):
+            acc = bank(6 + h, HALF)
+            product(acc[:], z_codes, z_scales, 0, z2_codes, z2_scales, halves[h])
+            leave_psum("scalar" if h == 0 else "vector", s[0][:, halves[h]], acc)
+        s_acc = {}
+        for t in range(1, PACK):
+            s_acc[t] = bank(t, S)
+            product(s_acc[t][:], z_codes, z_scales, t, z2_codes, z2_scales, whole)
 
         out_rows = out.rearrange("(p t) j -> t p j", t=PACK)
-        halves = [slice(0, HALF), slice(HALF, S)]
+        pa = sb("pa", [P, PACK, S], F32)
+        pb = sb("pb", [P, PACK, S], F32)
+        s_hi = sb("s_hi", [P, PACK, S], F32)
+        s_lo = sb("s_lo", [P, PACK, S], F32)
+        s_cut = sb("s_cut", [P, PACK, S], F32)
+        res = sb("res", [P, PACK, S], F32)
+
+        def s_first(t):
+            gather("scalar", pa[:, t, :], s[t], l6, whole)
+            nc.vector.tensor_tensor(s_hi[:, t, :], s[t][:, :S], pa[:, t, :], ALU.max)
+            nc.vector.tensor_tensor(s_lo[:, t, :], s[t][:, :S], pa[:, t, :], ALU.min)
+
+        for t in (1, 2):
+            leave_psum("vector", s[t][:, :S], s_acc[t])
         for t in range(PACK):
-            pa = sb("pa%d" % t, [P, S], F32)
-            pb = sb("pb%d" % t, [P, S], F32)
-            for h in range(2):
-                gather("scalar", pa[:, halves[h]], s[t], l6, h)
-            for h in range(2):
-                gather("scalar", pb[:, halves[h]], s[t], l7, h)
-            s_hi = sb("s_hi%d" % t, [P, S], F32)
-            s_lo = sb("s_lo%d" % t, [P, S], F32)
-            s_cut = sb("s_cut%d" % t, [P, S], F32)
-            res = sb("res%d" % t, [P, S], F32)
-            nc.vector.tensor_tensor(s_hi[:], s[t][:], pa[:], ALU.max)
-            nc.vector.tensor_tensor(s_lo[:], s[t][:], pa[:], ALU.min)
+            if t == 3:
+                leave_psum("scalar", s[t][:, :S], s_acc[t])
+            s_first(t)
+            for c in [whole] if t < PACK - 1 else halves:
+                gather("scalar", pb[:, t, c], s[t], l7, c)
             for c in halves:
-                nc.vector.tensor_tensor(s_cut[:, c], s_hi[:, c], pb[:, c], ALU.min)
+                nc.vector.tensor_tensor(s_cut[:, t, c], s_hi[:, t, c], pb[:, t, c], ALU.min)
             for c in halves:
-                nc.vector.tensor_tensor(res[:, c], s_lo[:, c], s_cut[:, c], ALU.max)
-                nc.sync.dma_start(out_rows[t][:, c], res[:, c])
+                nc.vector.tensor_tensor(res[:, t, c], s_lo[:, t, c], s_cut[:, t, c], ALU.max)
+            for c in [whole] if t < PACK - 1 else halves:
+                nc.sync.dma_start(out_rows[t][:, c], res[:, t, c])

@@ -20,7 +20,7 @@ PACK = 4
 HALF = S // 2
 LANES = 16
 WINDOW = 2 * S
-W_SPLIT = 64
+W_SPLIT = 48
 
 
 def tile_picked_selfprodtop2med_none_p_kernel(
@@ -31,8 +31,8 @@ def tile_picked_selfprodtop2med_none_p_kernel(
         keep = ctx.enter_context(tc.tile_pool(name="keep", bufs=1))
         psum = ctx.enter_context(tc.psum_pool(name="psum", bufs=1))
 
-        def sb(name, shape, dtype):
-            return keep.tile(shape, dtype, name=name, align_bytes=64)
+        def sb(name, shape, dtype, tag=None):
+            return keep.tile(shape, dtype, name=name, tag=tag or name, align_bytes=64)
 
         def load_list(name, src):
             lst = sb(name, [P, S // LANES], U16)
@@ -80,7 +80,7 @@ def tile_picked_selfprodtop2med_none_p_kernel(
         nc.scalar.copy(w_dst[:, W_SPLIT:], w_src[:, W_SPLIT:])
         xs_pick = sb("xs_pick", [P, S], U8)
         nc.vector.tensor_copy(xs_pick[:], xs[:].indirect(l_offs[:]))
-        w_codes = sb("w_codes", [P, H], U32)
+        w_codes = sb("w_codes", [P, H], U32, tag="xs")
         w_scales = sb("w_scales", [P, H], U8)
         nc.vector.quantize_mx(out=w_codes[:].bitcast(FP8X4), scales=w_scales[:], in_=w_bf[:])
         xw_pick = sb("xw_pick", [P, S], U32)
@@ -124,36 +124,35 @@ def tile_picked_selfprodtop2med_none_p_kernel(
         med = sb("med", [P, PACK, S], F32)
         mix = sb("mix", [P, PACK, S], F32)
 
-        def fetch(t):
+        def sort_pair(u):
+            nc.vector.tensor_tensor(hi[:, u, :], b1[:, u, :], b2[:, u, :], ALU.max)
+            nc.vector.tensor_tensor(lo[:, u, :], b1[:, u, :], b2[:, u, :], ALU.min)
+
+        def place_third(u):
+            nc.vector.tensor_tensor(cut[:, u, :], hi[:, u, :], b3[:, u, :], ALU.min)
+            nc.vector.tensor_tensor(top[:, u, :], hi[:, u, :], b3[:, u, :], ALU.max)
+            nc.vector.tensor_tensor(med[:, u, :], lo[:, u, :], cut[:, u, :], ALU.max)
+
+        def combine(u):
+            nc.vector.scalar_tensor_tensor(mix[:, u, :], med[:, u, :], -0.5, top[:, u, :], ALU.mult, ALU.add)
+
+        for t in range(2):
             gather("scalar", b1[:, t, :], y[t], l3, whole)
-            gather("vector" if t < 2 else "scalar", b2[:, t, :], y[t], l4, whole)
+            gather("vector", b2[:, t, :], y[t], l4, whole)
             gather("scalar", b3[:, t, :], y[t], l5, whole)
-
-        def sort_pair(t):
-            nc.vector.tensor_tensor(hi[:, t, :], b1[:, t, :], b2[:, t, :], ALU.max)
-            nc.vector.tensor_tensor(lo[:, t, :], b1[:, t, :], b2[:, t, :], ALU.min)
-
-        def place_third(t):
-            nc.vector.tensor_tensor(cut[:, t, :], hi[:, t, :], b3[:, t, :], ALU.min)
-            nc.vector.tensor_tensor(top[:, t, :], hi[:, t, :], b3[:, t, :], ALU.max)
-
-        def median(t):
-            nc.vector.tensor_tensor(med[:, t, :], lo[:, t, :], cut[:, t, :], ALU.max)
-
-        def combine(t):
-            nc.vector.scalar_tensor_tensor(mix[:, t, :], med[:, t, :], -0.5, top[:, t, :], ALU.mult, ALU.add)
-
-        for t in range(PACK):
-            if t == 3:
-                nc.scalar.copy(y[3][:, :S], y_acc[3][:])
-            fetch(t)
-            sort_pair(t)
+            sort_pair(slice(t, t + 1))
             if t == 0:
                 nc.vector.tensor_copy(y[2][:, :S], y_acc[2][:])
-            else:
-                combine(t - 1)
-            place_third(t)
-            median(t)
+            place_third(slice(t, t + 1))
+        nc.scalar.copy(y[3][:, :S], y_acc[3][:])
+        for t in (2, 3):
+            gather("scalar", b1[:, t, :], y[t], l3, whole)
+            gather("scalar", b2[:, t, :], y[t], l4, whole)
+        for t in (2, 3):
+            gather("scalar", b3[:, t, :], y[t], l5, whole)
+        combine(slice(0, 2))
+        sort_pair(slice(2, 4))
+        place_third(slice(2, 4))
 
         z_bf = sb("z_bf", [P, PACK, P * PACK], BF16)
         a1 = sb("a1", [P, PACK, S], F32)
@@ -172,7 +171,7 @@ def tile_picked_selfprodtop2med_none_p_kernel(
             )
 
         z_piece(0, whole)
-        combine(PACK - 1)
+        combine(slice(2, 4))
         z_piece(1, whole)
         nc.vector.tensor_tensor(
             z2_bf[:].rearrange("p (c i t) -> p c t i", i=4, t=PACK),
@@ -182,9 +181,10 @@ def tile_picked_selfprodtop2med_none_p_kernel(
         )
         z_piece(2, whole)
         nc.vector.quantize_mx(out=z2_codes[:].bitcast(FP8X4), scales=z2_scales[:], in_=z2_bf[:])
-        for c in halves:
-            z_piece(3, c)
-        z_deal(nc.scalar.copy, halves[0])
+        z_piece(3, halves[0])
+        z_deal(nc.vector.tensor_copy, slice(0, HALF // 2))
+        z_piece(3, halves[1])
+        z_deal(nc.scalar.copy, slice(HALF // 2, HALF))
         z_deal(nc.vector.tensor_copy, halves[1])
 
         z_codes = sb("z_codes", [P, S], U32)
@@ -215,22 +215,37 @@ def tile_picked_selfprodtop2med_none_p_kernel(
         s_cut = sb("s_cut", [P, PACK, S], F32)
         res = sb("res", [P, PACK, S], F32)
 
-        def s_first(t):
-            gather("scalar", pa[:, t, :], s[t], l6, whole)
+        last = PACK - 1
+
+        def upper(t):
             nc.vector.tensor_tensor(s_hi[:, t, :], s[t][:, :S], pa[:, t, :], ALU.max)
+
+        def lower(t):
             nc.vector.tensor_tensor(s_lo[:, t, :], s[t][:, :S], pa[:, t, :], ALU.min)
+
+        def cap(t, c):
+            nc.vector.tensor_tensor(s_cut[:, t, c], s_hi[:, t, c], pb[:, t, c], ALU.min)
+
+        def finish(t, c):
+            nc.vector.tensor_tensor(res[:, t, c], s_lo[:, t, c], s_cut[:, t, c], ALU.max)
+            nc.sync.dma_start(out_rows[t][:, c], res[:, t, c])
 
         for t in (1, 2):
             leave_psum("vector", s[t][:, :S], s_acc[t])
-        for t in range(PACK):
-            if t == 3:
-                leave_psum("scalar", s[t][:, :S], s_acc[t])
-            s_first(t)
-            for c in [whole] if t < PACK - 1 else halves:
-                gather("scalar", pb[:, t, c], s[t], l7, c)
-            for c in halves:
-                nc.vector.tensor_tensor(s_cut[:, t, c], s_hi[:, t, c], pb[:, t, c], ALU.min)
-            for c in halves:
-                nc.vector.tensor_tensor(res[:, t, c], s_lo[:, t, c], s_cut[:, t, c], ALU.max)
-            for c in [whole] if t < PACK - 1 else halves:
-                nc.sync.dma_start(out_rows[t][:, c], res[:, t, c])
+        gather("scalar", pa[:, 0, :], s[0], l6, whole)
+        upper(0)
+        for t in range(last):
+            lower(t)
+            gather("scalar", pb[:, t, :], s[t], l7, whole)
+            cap(t, whole)
+            if t == 0:
+                leave_psum("vector", s[last][:, :S], s_acc[last])
+            gather("scalar", pa[:, t + 1, :], s[t + 1], l6, whole)
+            upper(t + 1)
+            finish(t, whole)
+        lower(last)
+        for c in halves:
+            gather("scalar", pb[:, last, c], s[last], l7, c)
+            cap(last, c)
+        for c in halves:
+            finish(last, c)

@@ -17,10 +17,12 @@ COPY = mybir.ActivationFunctionType.Copy
 
 P = 128
 PACK = 4
-HALF = S // 2
 LANES = 16
+QUADRANT = 32
+HALF = S // 2
 WINDOW = 2 * S
 W_SPLIT = 48
+S_FACTOR = 0.0625
 
 
 def tile_picked_selfprodtop2med_none_p_kernel(
@@ -34,27 +36,40 @@ def tile_picked_selfprodtop2med_none_p_kernel(
         def sb(name, shape, dtype, tag=None):
             return keep.tile(shape, dtype, name=name, tag=tag or name, align_bytes=64)
 
+        def bank(b, width):
+            return psum.tile([P, width], F32, name="bank%d" % b, tag="bank%d" % b)
+
         def load_list(name, src):
             lst = sb(name, [P, S // LANES], U16)
             nc.sync.dma_start(lst[:], src)
             return lst
 
-        def gather(engine, dst, window, lst, cols):
-            picked = window[:].indirect(lst[:, cols.start // LANES : cols.stop // LANES])
+        def gather(engine, dst, window, lst, entries):
+            picked = window[:].indirect(lst[:, entries.start // LANES : entries.stop // LANES])
             if engine == "scalar":
                 nc.scalar.activation(dst, picked, COPY)
             else:
                 nc.vector.tensor_copy(dst, picked)
 
+        def product(acc, codes, scales, t, rhs, rhs_scales, cols):
+            rows = slice(t * P, (t + 1) * P)
+            nc.tensor.matmul_mx(
+                out=acc, lhsT=codes[:, rows].bitcast(FP8X4), lhsT_scale=scales[:, rows],
+                rhs=rhs[:, cols].bitcast(FP8X4), rhs_scale=rhs_scales[:, cols], start=True, stop=True,
+            )
+
         whole = slice(0, S)
         halves = [slice(0, HALF), slice(HALF, S)]
+        last = PACK - 1
 
         xs = sb("xs", [P, T], U8)
         nc.gpsimd.memset(xs[:].bitcast(U32), 0)
         w_raw = sb("w_raw", [P, PACK, H], F32)
         nc.sync.dma_start(w_raw[:], w1.rearrange("(p j) c -> p j c", j=PACK))
-        for q in range(4):
-            nc.sync.dma_start(xs[32 * q : 32 * q + 4, :].bitcast(I32), x_scales[0, 4 * q : 4 * q + 4, :].bitcast(I32))
+        for q in range(P // QUADRANT):
+            nc.sync.dma_start(
+                xs[QUADRANT * q : QUADRANT * q + 4, :].bitcast(I32), x_scales[0, 4 * q : 4 * q + 4, :].bitcast(I32)
+            )
         l_offs = load_list("l_offs", offs)
         xw = sb("xw", [P, T], U32)
         nc.sync.dma_start(xw[:].bitcast(I32), x_words[0].rearrange("p n r -> p (n r)").bitcast(I32))
@@ -79,23 +94,13 @@ def tile_picked_selfprodtop2med_none_p_kernel(
         nc.vector.tensor_copy(w_dst[:, :W_SPLIT], w_src[:, :W_SPLIT])
         nc.scalar.copy(w_dst[:, W_SPLIT:], w_src[:, W_SPLIT:])
         xs_pick = sb("xs_pick", [P, S], U8)
-        nc.vector.tensor_copy(xs_pick[:], xs[:].indirect(l_offs[:]))
+        gather("vector", xs_pick[:], xs, l_offs, whole)
         w_codes = sb("w_codes", [P, H], U32, tag="xs")
         w_scales = sb("w_scales", [P, H], U8)
         nc.vector.quantize_mx(out=w_codes[:].bitcast(FP8X4), scales=w_scales[:], in_=w_bf[:])
         xw_pick = sb("xw_pick", [P, S], U32)
-        for c in halves:
-            gather("vector", xw_pick[:, c], xw, l_offs, c)
-
-        def product(acc, codes, scales, t, rhs, rhs_scales, c):
-            cols = slice(t * P, (t + 1) * P)
-            nc.tensor.matmul_mx(
-                out=acc, lhsT=codes[:, cols].bitcast(FP8X4), lhsT_scale=scales[:, cols],
-                rhs=rhs[:, c].bitcast(FP8X4), rhs_scale=rhs_scales[:, c], start=True, stop=True,
-            )
-
-        def bank(b, width):
-            return psum.tile([P, width], F32, name="bank%d" % b, tag="bank%d" % b)
+        for cols in halves:
+            gather("vector", xw_pick[:, cols], xw, l_offs, cols)
 
         for h in range(2):
             for t in range(2):
@@ -113,7 +118,6 @@ def tile_picked_selfprodtop2med_none_p_kernel(
         z2_bf = sb("z2_bf", [P, S * PACK], BF16)
         z2_codes = sb("z2_codes", [P, S], U32)
         z2_scales = sb("z2_scales", [P, S], U8)
-        gb_wide = gb_sb[:].rearrange("p (c t i) -> p c t i", c=1, i=1).to_broadcast([P, S // 4, PACK, 4])
         b1 = sb("b1", [P, PACK, S], F32)
         b2 = sb("b2", [P, PACK, S], F32)
         b3 = sb("b3", [P, PACK, S], F32)
@@ -124,17 +128,19 @@ def tile_picked_selfprodtop2med_none_p_kernel(
         med = sb("med", [P, PACK, S], F32)
         mix = sb("mix", [P, PACK, S], F32)
 
-        def sort_pair(u):
-            nc.vector.tensor_tensor(hi[:, u, :], b1[:, u, :], b2[:, u, :], ALU.max)
-            nc.vector.tensor_tensor(lo[:, u, :], b1[:, u, :], b2[:, u, :], ALU.min)
+        def sort_pair(tiles):
+            nc.vector.tensor_tensor(hi[:, tiles, :], b1[:, tiles, :], b2[:, tiles, :], ALU.max)
+            nc.vector.tensor_tensor(lo[:, tiles, :], b1[:, tiles, :], b2[:, tiles, :], ALU.min)
 
-        def place_third(u):
-            nc.vector.tensor_tensor(cut[:, u, :], hi[:, u, :], b3[:, u, :], ALU.min)
-            nc.vector.tensor_tensor(top[:, u, :], hi[:, u, :], b3[:, u, :], ALU.max)
-            nc.vector.tensor_tensor(med[:, u, :], lo[:, u, :], cut[:, u, :], ALU.max)
+        def place_third(tiles):
+            nc.vector.tensor_tensor(cut[:, tiles, :], hi[:, tiles, :], b3[:, tiles, :], ALU.min)
+            nc.vector.tensor_tensor(top[:, tiles, :], hi[:, tiles, :], b3[:, tiles, :], ALU.max)
+            nc.vector.tensor_tensor(med[:, tiles, :], lo[:, tiles, :], cut[:, tiles, :], ALU.max)
 
-        def combine(u):
-            nc.vector.scalar_tensor_tensor(mix[:, u, :], med[:, u, :], -0.5, top[:, u, :], ALU.mult, ALU.add)
+        def combine(tiles):
+            nc.vector.scalar_tensor_tensor(
+                mix[:, tiles, :], med[:, tiles, :], -0.5, top[:, tiles, :], ALU.mult, ALU.add
+            )
 
         for t in range(2):
             gather("scalar", b1[:, t, :], y[t], l3, whole)
@@ -145,11 +151,12 @@ def tile_picked_selfprodtop2med_none_p_kernel(
                 nc.vector.tensor_copy(y[2][:, :S], y_acc[2][:])
             place_third(slice(t, t + 1))
         nc.scalar.copy(y[3][:, :S], y_acc[3][:])
-        for t in (2, 3):
-            gather("scalar", b1[:, t, :], y[t], l3, whole)
-            gather("scalar", b2[:, t, :], y[t], l4, whole)
+        gather("scalar", b1[:, 2, :], y[2], l3, whole)
+        gather("scalar", b2[:, 2, :], y[2], l4, whole)
+        gather("scalar", b1[:, 3, :], y[3], l3, whole)
         for t in (2, 3):
             gather("scalar", b3[:, t, :], y[t], l5, whole)
+        gather("vector", b2[:, 3, :], y[3], l4, whole)
         combine(slice(0, 2))
         sort_pair(slice(2, 4))
         place_third(slice(2, 4))
@@ -159,44 +166,46 @@ def tile_picked_selfprodtop2med_none_p_kernel(
         a2 = sb("a2", [P, PACK, S], F32)
         z_rows = sb("z_rows", [P, PACK, S], BF16)
 
-        def z_piece(t, c):
-            gather("scalar", a1[:, t, c], y[t], l1, c)
-            gather("scalar", a2[:, t, c], y[t], l2, c)
-            nc.vector.scalar_tensor_tensor(z_rows[:, t, c], a1[:, t, c], ga_sb[:, t : t + 1], a2[:, t, c], ALU.mult, ALU.mult)
+        def z_piece(t, cols):
+            gather("scalar", a1[:, t, cols], y[t], l1, cols)
+            gather("scalar", a2[:, t, cols], y[t], l2, cols)
+            nc.vector.scalar_tensor_tensor(
+                z_rows[:, t, cols], a1[:, t, cols], ga_sb[:, t : t + 1], a2[:, t, cols], ALU.mult, ALU.mult
+            )
 
-        def z_deal(copy, c):
+        def z_deal(copy, cols):
             copy(
-                z_bf[:, :, c].rearrange("p i (c e t) -> p c t e i", e=2, t=PACK),
-                z_rows[:, :, c].rearrange("p t (c e i) -> p c t e i", e=2, i=4),
+                z_bf[:, :, cols].rearrange("p i (g e t) -> p g t e i", e=2, t=PACK),
+                z_rows[:, :, cols].rearrange("p t (g e i) -> p g t e i", e=2, i=PACK),
             )
 
         z_piece(0, whole)
         combine(slice(2, 4))
         z_piece(1, whole)
         nc.vector.tensor_tensor(
-            z2_bf[:].rearrange("p (c i t) -> p c t i", i=4, t=PACK),
-            mix[:].rearrange("p t (c i) -> p c t i", i=4),
-            gb_wide,
+            z2_bf[:].rearrange("p (g i t) -> p g t i", i=4, t=PACK),
+            mix[:].rearrange("p t (g i) -> p g t i", i=4),
+            gb_sb[:].rearrange("p (g t i) -> p g t i", g=1, i=1).to_broadcast([P, S // 4, PACK, 4]),
             ALU.mult,
         )
         z_piece(2, whole)
+        for cols in halves:
+            z_piece(last, cols)
+        z_deal(nc.scalar.copy, halves[0])
         nc.vector.quantize_mx(out=z2_codes[:].bitcast(FP8X4), scales=z2_scales[:], in_=z2_bf[:])
-        z_piece(3, halves[0])
-        z_deal(nc.vector.tensor_copy, slice(0, HALF // 2))
-        z_piece(3, halves[1])
-        z_deal(nc.scalar.copy, slice(HALF // 2, HALF))
         z_deal(nc.vector.tensor_copy, halves[1])
 
         z_codes = sb("z_codes", [P, S], U32)
         z_scales = sb("z_scales", [P, S], U8)
         for t in range(PACK):
-            cols = slice(t * P, (t + 1) * P)
-            nc.vector.quantize_mx(out=z_codes[:, cols].bitcast(FP8X4), scales=z_scales[:, cols], in_=z_bf[:, t, :])
+            rows = slice(t * P, (t + 1) * P)
+            nc.vector.quantize_mx(out=z_codes[:, rows].bitcast(FP8X4), scales=z_scales[:, rows], in_=z_bf[:, t, :])
+
         def leave_psum(engine, dst, acc):
             if engine == "scalar":
-                nc.scalar.activation(dst, acc[:], COPY, scale=0.0625)
+                nc.scalar.activation(dst, acc[:], COPY, scale=S_FACTOR)
             else:
-                nc.vector.tensor_scalar(dst, acc[:], 0.0625, None, ALU.mult)
+                nc.vector.tensor_scalar(dst, acc[:], S_FACTOR, None, ALU.mult)
 
         for h in range(2):
             acc = bank(6 + h, HALF)
@@ -215,37 +224,46 @@ def tile_picked_selfprodtop2med_none_p_kernel(
         s_cut = sb("s_cut", [P, PACK, S], F32)
         res = sb("res", [P, PACK, S], F32)
 
-        last = PACK - 1
-
         def upper(t):
+            gather("scalar", pa[:, t, :], s[t], l6, whole)
             nc.vector.tensor_tensor(s_hi[:, t, :], s[t][:, :S], pa[:, t, :], ALU.max)
 
         def lower(t):
             nc.vector.tensor_tensor(s_lo[:, t, :], s[t][:, :S], pa[:, t, :], ALU.min)
 
-        def cap(t, c):
-            nc.vector.tensor_tensor(s_cut[:, t, c], s_hi[:, t, c], pb[:, t, c], ALU.min)
+        def cap(t, cols):
+            nc.vector.tensor_tensor(s_cut[:, t, cols], s_hi[:, t, cols], pb[:, t, cols], ALU.min)
 
-        def finish(t, c):
-            nc.vector.tensor_tensor(res[:, t, c], s_lo[:, t, c], s_cut[:, t, c], ALU.max)
-            nc.sync.dma_start(out_rows[t][:, c], res[:, t, c])
+        def finish(t, cols):
+            nc.vector.tensor_tensor(res[:, t, cols], s_lo[:, t, cols], s_cut[:, t, cols], ALU.max)
+
+        def store(t, cols):
+            nc.sync.dma_start(out_rows[t][:, cols], res[:, t, cols])
 
         for t in (1, 2):
             leave_psum("vector", s[t][:, :S], s_acc[t])
-        gather("scalar", pa[:, 0, :], s[0], l6, whole)
         upper(0)
-        for t in range(last):
+        for t in range(2):
             lower(t)
             gather("scalar", pb[:, t, :], s[t], l7, whole)
             cap(t, whole)
             if t == 0:
                 leave_psum("vector", s[last][:, :S], s_acc[last])
-            gather("scalar", pa[:, t + 1, :], s[t + 1], l6, whole)
             upper(t + 1)
             finish(t, whole)
+            store(t, whole)
+        lower(2)
+        gather("scalar", pb[:, 2, :], s[2], l7, whole)
+        for cols in halves:
+            cap(2, cols)
+        for cols in halves:
+            finish(2, cols)
+        store(2, whole)
+        upper(last)
         lower(last)
-        for c in halves:
-            gather("scalar", pb[:, last, c], s[last], l7, c)
-            cap(last, c)
-        for c in halves:
-            finish(last, c)
+        for cols in halves:
+            gather("scalar", pb[:, last, cols], s[last], l7, cols)
+            cap(last, cols)
+        for cols in halves:
+            finish(last, cols)
+            store(last, cols)

from contextlib import ExitStack

import concourse.mybir as mybir

K, T, S, H = 512, 2048, 512, 512
FLOPS = 2 * K * H * S + 2 * H * S * S

F32 = mybir.dt.float32
BF16 = mybir.dt.bfloat16
I32 = mybir.dt.int32
U32 = mybir.dt.uint32
U16 = mybir.dt.uint16
U8 = mybir.dt.uint8
FP8X4 = mybir.dt.float8_e4m3fn_x4
ALU = mybir.AluOpType
COPY = mybir.ActivationFunctionType.Copy

P = 128
PACK = 4
LANES = 16
QUADRANT = 32
HALF = S // 2
WINDOW = 2 * S
W_SPLIT = 48
S_FACTOR = 0.0625


def tile_picked_selfprodtop2med_none_p_kernel(
    tc, x_words, x_scales, w1, ga, gb, offs, n1, n2, n3, n4, n5, n6, n7, out
):
    nc = tc.nc
    with ExitStack() as ctx:
        keep = ctx.enter_context(tc.tile_pool(name="keep", bufs=1))
        psum = ctx.enter_context(tc.psum_pool(name="psum", bufs=1))

        def sb(name, shape, dtype, tag=None):
            return keep.tile(shape, dtype, name=name, tag=tag or name, align_bytes=64)

        def bank(b, width):
            return psum.tile([P, width], F32, name="bank%d" % b, tag="bank%d" % b)

        def load_list(name, src):
            lst = sb(name, [P, S // LANES], U16)
            nc.sync.dma_start(lst[:], src)
            return lst

        def gather(engine, dst, window, lst, entries):
            picked = window[:].indirect(lst[:, entries.start // LANES : entries.stop // LANES])
            if engine == "scalar":
                nc.scalar.activation(dst, picked, COPY)
            else:
                nc.vector.tensor_copy(dst, picked)

        def product(acc, codes, scales, t, rhs, rhs_scales, cols):
            rows = slice(t * P, (t + 1) * P)
            nc.tensor.matmul_mx(
                out=acc, lhsT=codes[:, rows].bitcast(FP8X4), lhsT_scale=scales[:, rows],
                rhs=rhs[:, cols].bitcast(FP8X4), rhs_scale=rhs_scales[:, cols], start=True, stop=True,
            )

        whole = slice(0, S)
        halves = [slice(0, HALF), slice(HALF, S)]
        last = PACK - 1

        xs = sb("xs", [P, T], U8)
        nc.gpsimd.memset(xs[:].bitcast(U32), 0)
        w_raw = sb("w_raw", [P, PACK, H], F32)
        nc.sync.dma_start(w_raw[:], w1.rearrange("(p j) c -> p j c", j=PACK))
        for q in range(P // QUADRANT):
            nc.sync.dma_start(
                xs[QUADRANT * q : QUADRANT * q + 4, :].bitcast(I32), x_scales[0, 4 * q : 4 * q + 4, :].bitcast(I32)
            )
        l_offs = load_list("l_offs", offs)
        xw = sb("xw", [P, T], U32)
        nc.sync.dma_start(xw[:].bitcast(I32), x_words[0].rearrange("p n r -> p (n r)").bitcast(I32))
        l3 = load_list("l3", n3)
        l4 = load_list("l4", n4)
        l5 = load_list("l5", n5)
        l1 = load_list("l1", n1)
        l2 = load_list("l2", n2)
        ga_sb = sb("ga_sb", [P, PACK], F32)
        gb_sb = sb("gb_sb", [P, PACK], F32)
        nc.sync.dma_start(gb_sb[:], gb.rearrange("(p t) o -> p (t o)", t=PACK))
        nc.sync.dma_start(ga_sb[:], ga.rearrange("(p t) o -> p (t o)", t=PACK))
        l6 = load_list("l6", n6)
        l7 = load_list("l7", n7)

        y = [sb("y%d" % t, [P, WINDOW], F32) for t in range(PACK)]
        s = [sb("s%d" % t, [P, WINDOW], F32) for t in range(PACK)]

        w_bf = sb("w_bf", [P, H * PACK], BF16)
        w_dst = w_bf[:].rearrange("p (t m j) -> p m j t", t=PACK, j=PACK)
        w_src = w_raw[:].rearrange("p j (m t) -> p m j t", t=PACK)
        nc.vector.tensor_copy(w_dst[:, :W_SPLIT], w_src[:, :W_SPLIT])
        nc.scalar.copy(w_dst[:, W_SPLIT:], w_src[:, W_SPLIT:])
        xs_pick = sb("xs_pick", [P, S], U8)
        gather("vector", xs_pick[:], xs, l_offs, whole)
        w_codes = sb("w_codes", [P, H], U32, tag="xs")
        w_scales = sb("w_scales", [P, H], U8)
        nc.vector.quantize_mx(out=w_codes[:].bitcast(FP8X4), scales=w_scales[:], in_=w_bf[:])
        xw_pick = sb("xw_pick", [P, S], U32)
        for cols in halves:
            gather("vector", xw_pick[:, cols], xw, l_offs, cols)

        for h in range(2):
            for t in range(2):
                acc = bank(2 * h + t, HALF)
                product(acc[:], w_codes, w_scales, t, xw_pick, xs_pick, halves[h])
                if t == 0:
                    nc.scalar.copy(y[t][:, halves[h]], acc[:])
                else:
                    nc.vector.tensor_copy(y[t][:, halves[h]], acc[:])
        y_acc = {}
        for t in range(2, PACK):
            y_acc[t] = bank(2 + t, S)
            product(y_acc[t][:], w_codes, w_scales, t, xw_pick, xs_pick, whole)

        z2_bf = sb("z2_bf", [P, S * PACK], BF16)
        z2_codes = sb("z2_codes", [P, S], U32)
        z2_scales = sb("z2_scales", [P, S], U8)
        b1 = sb("b1", [P, PACK, S], F32)
        b2 = sb("b2", [P, PACK, S], F32)
        b3 = sb("b3", [P, PACK, S], F32)
        hi = sb("hi", [P, PACK, S], F32)
        lo = sb("lo", [P, PACK, S], F32)
        top = sb("top", [P, PACK, S], F32)
        cut = sb("cut", [P, PACK, S], F32)
        med = sb("med", [P, PACK, S], F32)
        mix = sb("mix", [P, PACK, S], F32)

        def sort_pair(tiles):
            nc.vector.tensor_tensor(hi[:, tiles, :], b1[:, tiles, :], b2[:, tiles, :], ALU.max)
            nc.vector.tensor_tensor(lo[:, tiles, :], b1[:, tiles, :], b2[:, tiles, :], ALU.min)

        def place_third(tiles):
            nc.vector.tensor_tensor(cut[:, tiles, :], hi[:, tiles, :], b3[:, tiles, :], ALU.min)
            nc.vector.tensor_tensor(top[:, tiles, :], hi[:, tiles, :], b3[:, tiles, :], ALU.max)
            nc.vector.tensor_tensor(med[:, tiles, :], lo[:, tiles, :], cut[:, tiles, :], ALU.max)

        def combine(tiles):
            nc.vector.scalar_tensor_tensor(
                mix[:, tiles, :], med[:, tiles, :], -0.5, top[:, tiles, :], ALU.mult, ALU.add
            )

        for t in range(2):
            gather("scalar", b1[:, t, :], y[t], l3, whole)
            gather("vector", b2[:, t, :], y[t], l4, whole)
            gather("scalar", b3[:, t, :], y[t], l5, whole)
            sort_pair(slice(t, t + 1))
            if t == 0:
                nc.vector.tensor_copy(y[2][:, :S], y_acc[2][:])
            place_third(slice(t, t + 1))
        nc.scalar.copy(y[3][:, :S], y_acc[3][:])
        gather("scalar", b1[:, 2, :], y[2], l3, whole)
        gather("scalar", b2[:, 2, :], y[2], l4, whole)
        gather("scalar", b1[:, 3, :], y[3], l3, whole)
        for t in (2, 3):
            gather("scalar", b3[:, t, :], y[t], l5, whole)
        gather("vector", b2[:, 3, :], y[3], l4, whole)
        combine(slice(0, 2))
        sort_pair(slice(2, 4))
        place_third(slice(2, 4))

        z_bf = sb("z_bf", [P, PACK, P * PACK], BF16)
        a1 = sb("a1", [P, PACK, S], F32)
        a2 = sb("a2", [P, PACK, S], F32)
        z_rows = sb("z_rows", [P, PACK, S], BF16)

        def z_piece(t, cols):
            gather("scalar", a1[:, t, cols], y[t], l1, cols)
            gather("scalar", a2[:, t, cols], y[t], l2, cols)
            nc.vector.scalar_tensor_tensor(
                z_rows[:, t, cols], a1[:, t, cols], ga_sb[:, t : t + 1], a2[:, t, cols], ALU.mult, ALU.mult
            )

        def z_deal(copy, cols):
            copy(
                z_bf[:, :, cols].rearrange("p i (g e t) -> p g t e i", e=2, t=PACK),
                z_rows[:, :, cols].rearrange("p t (g e i) -> p g t e i", e=2, i=PACK),
            )

        z_piece(0, whole)
        combine(slice(2, 4))
        z_piece(1, whole)
        nc.vector.tensor_tensor(
            z2_bf[:].rearrange("p (g i t) -> p g t i", i=4, t=PACK),
            mix[:].rearrange("p t (g i) -> p g t i", i=4),
            gb_sb[:].rearrange("p (g t i) -> p g t i", g=1, i=1).to_broadcast([P, S // 4, PACK, 4]),
            ALU.mult,
        )
        z_piece(2, whole)
        for cols in halves:
            z_piece(last, cols)
        z_deal(nc.scalar.copy, halves[0])
        nc.vector.quantize_mx(out=z2_codes[:].bitcast(FP8X4), scales=z2_scales[:], in_=z2_bf[:])
        z_deal(nc.vector.tensor_copy, halves[1])

        z_codes = sb("z_codes", [P, S], U32)
        z_scales = sb("z_scales", [P, S], U8)
        for t in range(PACK):
            rows = slice(t * P, (t + 1) * P)
            nc.vector.quantize_mx(out=z_codes[:, rows].bitcast(FP8X4), scales=z_scales[:, rows], in_=z_bf[:, t, :])

        def leave_psum(engine, dst, acc):
            if engine == "scalar":
                nc.scalar.activation(dst, acc[:], COPY, scale=S_FACTOR)
            else:
                nc.vector.tensor_scalar(dst, acc[:], S_FACTOR, None, ALU.mult)

        for h in range(2):
            acc = bank(6 + h, HALF)
            product(acc[:], z_codes, z_scales, 0, z2_codes, z2_scales, halves[h])
            leave_psum("scalar" if h == 0 else "vector", s[0][:, halves[h]], acc)
        s_acc = {}
        for t in range(1, PACK):
            s_acc[t] = bank(t, S)
            product(s_acc[t][:], z_codes, z_scales, t, z2_codes, z2_scales, whole)

        out_rows = out.rearrange("(p t) j -> t p j", t=PACK)
        pa = sb("pa", [P, PACK, S], F32)
        pb = sb("pb", [P, PACK, S], F32)
        s_hi = sb("s_hi", [P, PACK, S], F32)
        s_lo = sb("s_lo", [P, PACK, S], F32)
        s_cut = sb("s_cut", [P, PACK, S], F32)
        res = sb("res", [P, PACK, S], F32)

        def upper(t):
            gather("scalar", pa[:, t, :], s[t], l6, whole)
            nc.vector.tensor_tensor(s_hi[:, t, :], s[t][:, :S], pa[:, t, :], ALU.max)

        def lower(t):
            nc.vector.tensor_tensor(s_lo[:, t, :], s[t][:, :S], pa[:, t, :], ALU.min)

        def cap(t, cols):
            nc.vector.tensor_tensor(s_cut[:, t, cols], s_hi[:, t, cols], pb[:, t, cols], ALU.min)

        def finish(t, cols):
            nc.vector.tensor_tensor(res[:, t, cols], s_lo[:, t, cols], s_cut[:, t, cols], ALU.max)

        def store(t, cols):
            nc.sync.dma_start(out_rows[t][:, cols], res[:, t, cols])

        for t in (1, 2):
            leave_psum("vector", s[t][:, :S], s_acc[t])
        upper(0)
        for t in range(2):
            lower(t)
            gather("scalar", pb[:, t, :], s[t], l7, whole)
            cap(t, whole)
            if t == 0:
                leave_psum("vector", s[last][:, :S], s_acc[last])
            upper(t + 1)
            finish(t, whole)
            store(t, whole)
        lower(2)
        gather("scalar", pb[:, 2, :], s[2], l7, whole)
        for cols in halves:
            cap(2, cols)
        for cols in halves:
            finish(2, cols)
        store(2, whole)
        upper(last)
        lower(last)
        for cols in halves:
            gather("scalar", pb[:, last, cols], s[last], l7, cols)
            cap(last, cols)
        for cols in halves:
            finish(last, cols)
            store(last, cols)
